import numpy as np
import ml_dtypes


def mxq(x, axis, fmt="e4m3"):
    dtype, down = {"e4m3": (ml_dtypes.float8_e4m3fn, 7), "e5m2": (ml_dtypes.float8_e5m2, 14)}[fmt]
    v = np.moveaxis(np.asarray(x, np.float32).astype(ml_dtypes.bfloat16).astype(np.float64), axis, -1)
    blocks = v.reshape(v.shape[:-1] + (-1, 32))
    amax = np.abs(blocks).max(-1, keepdims=True)
    byte = np.maximum(np.where(amax > 0, np.frexp(amax)[1] - 1 + 127, 0) - down, 1)
    scale = np.exp2(byte - 127.0)
    codes = (blocks / scale).astype(np.float32).astype(dtype).astype(np.float64)
    return np.moveaxis((codes * scale).reshape(v.shape), -1, axis)


WIDE = False


def mx_kscale(k):
    if not WIDE:
        return np.ones(k)
    levels = np.array([10, -10, 5, -5, 0])
    if k % 512:
        return np.exp2(np.random.permutation(np.resize(levels, k // 32))).repeat(32)
    a = np.empty((k // 512, 16))
    for p in range(k // 512):
        a[p, :8] = np.random.permutation(np.resize(levels, 8))
        for g in range(8):
            far = levels[np.abs(levels - a[p, g]) >= 10]
            a[p, g + 8] = far[np.random.randint(len(far))]
    return np.exp2(a.ravel()).repeat(32)


def f64(x):
    return np.asarray(x).astype(np.float64)


def striped(idx):
    return np.tile(idx.reshape(-1, 16).T, (8, 1)).astype(np.uint16)


def unstriped(offs):
    return offs[:16].T.reshape(-1).astype(np.int64)


E2M1 = np.array([0.0, 0.5, 1.0, 1.5, 2.0, 3.0, 4.0, 6.0, -0.0, -0.5, -1.0, -1.5, -2.0, -3.0, -4.0, -6.0])


def pack_weight(w, fmt):
    k, n = w.shape
    w = f64(np.asarray(w, np.float32).astype(ml_dtypes.bfloat16)).reshape(k // 32, 32, n)
    amax = np.abs(w).max(1)
    if fmt == "e4m3":
        byte = np.frexp(amax)[1] - 1 + 127 - 7
    else:
        mant, ex = np.frexp(amax / 6.0)
        byte = np.where(mant > 0.5, ex, ex - 1) + 127
    byte = np.clip(np.where(amax > 0, byte, 1), 1, 254)
    scaled = (w * np.exp2(127.0 - byte)[:, None, :]).reshape(k, n).astype(np.float32)
    by_word = np.ascontiguousarray(scaled.reshape(k // 512, 128, 4, n).transpose(0, 1, 3, 2))
    if fmt == "e4m3":
        words = by_word.astype(ml_dtypes.float8_e4m3fn).view(np.uint8)
    else:
        c = by_word.astype(ml_dtypes.float4_e2m1fn).view(np.uint8) & 0xF
        words = (c[..., 0::2] | (c[..., 1::2] << 4)).reshape(k // 512, 128, 2 * n)
    return np.ascontiguousarray(words), np.ascontiguousarray(byte.astype(np.uint8).reshape(k // 512, 16, n))


def unpack_weight(words, scales, fmt):
    g, _, n = scales.shape
    words = np.ascontiguousarray(words).reshape(g, 128, n, -1)
    if fmt == "e4m3":
        vals = words.view(ml_dtypes.float8_e4m3fn).astype(np.float64)
    else:
        nib = np.empty((g, 128, n, 4), np.uint8)
        nib[..., 0::2] = words & 0xF
        nib[..., 1::2] = words >> 4
        vals = E2M1[nib]
    vals = vals * np.repeat(np.exp2(scales.astype(np.float64) - 127.0), 8, axis=1)[..., None]
    return vals.transpose(0, 1, 3, 2).reshape(g * 512, n)


def gelu(v):
    return 0.5 * v * (1.0 + np.tanh(np.sqrt(2.0 / np.pi) * (v + 0.044715 * v**3)))


def bf(x):
    return np.asarray(x, np.float32).astype(ml_dtypes.bfloat16)


def planes(Y):
    n, m = Y.shape
    b = f64(bf(Y)).reshape(n // 32, 32, m)
    amax = np.abs(b).max(1)
    byte = np.clip(np.where(amax > 0, np.frexp(amax)[1] - 1 + 127 - 7, 1), 1, 254)
    codes = (b * np.exp2(127.0 - byte)[:, None, :]).reshape(n, m).astype(np.float32).astype(ml_dtypes.float8_e4m3fn).view(np.uint8)
    words = codes.reshape(n // 512, 128, 4, m).transpose(0, 1, 3, 2)
    return np.ascontiguousarray(words), np.ascontiguousarray(byte.astype(np.uint8).reshape(n // 512, 16, m))


K, T, S, T2, P, H, N = 1024, 2048, 512, 1024, 512, 1024, 512

def setup_inputs():
    n = np.random.standard_normal
    s = mx_kscale(K)[:, None]
    u = mx_kscale(H)[:, None]
    tab_words, tab_scales = pack_weight(n((K, T)) * s, "e4m3")
    w1_words, w1_scales = pack_weight(0.46 * n((K, H)) / np.sqrt(K) / s, "e2m1")
    w2 = 0.46 * n((K, H)) / np.sqrt(K) / s
    w3 = 2.0 * n((H, N)) / np.sqrt(H) / u * np.exp(0.8 * n(N))[None, :]
    w4_words, w4_scales = pack_weight(2.0 * n((H, N)) / np.sqrt(H) / u, "e4m3")
    gain = np.sign(n(H)) * np.random.uniform(2.0, 5.0, H) * u[:, 0]
    return {
        "tab_words": tab_words, "tab_scales": tab_scales,
        "offs": striped(np.random.permutation(T)[:S]),
        "offs2": striped(np.random.permutation(T2)[:S]),
        "offs3": striped(np.random.permutation(T2)[:P]),
        "w1_words": w1_words, "w1_scales": w1_scales,
        "w2": w2.astype(np.float32),
        "slope": np.random.uniform(0.5, 1.5, (H, S)).astype(np.float32),
        "page0": (0.8 * n((H, T2))).astype(np.float32),
        "wgs": np.exp(0.3 * n((128, S))).astype(np.float32),
        "gain": gain.astype(np.float32),
        "w3": w3.astype(np.float32),
        "w4_words": w4_words, "w4_scales": w4_scales,
    }

def reference(tab_words, tab_scales, offs, offs2, offs3, w1_words, w1_scales, w2,
              slope, page0, wgs, gain, w3, w4_words, w4_scales):
    v = unpack_weight(tab_words, tab_scales, "e4m3")[:, unstriped(offs)]
    w1 = unpack_weight(w1_words, w1_scales, "e2m1")
    w4 = unpack_weight(w4_words, w4_scales, "e4m3")
    wear = w1.T @ v
    mend = mxq(f64(w2), 0, "e4m3").T @ v
    h = (wear - mend) * f64(slope)
    page = f64(page0).copy()
    page[:, unstriped(offs2)] = np.tile(f64(wgs), (H // 128, 1)) * h
    top = page.max(axis=1)
    a = np.exp(page[:, unstriped(offs3)] - top[:, None])
    x = mxq(f64(gain)[:, None] * a, 0, "e4m3")
    y = (mxq(f64(w3), 0, "e4m3").T @ x) * (w4.T @ x)
    words, scales = planes(y)
    return y, words, scales

@@ -1,0 +1,355 @@
+from contextlib import ExitStack
+
+import concourse.mybir as mybir
+
+K, T, S, T2, M_OUT, H, N = 1024, 2048, 512, 1024, 512, 1024, 512
+FLOPS = 2 * (2 * K * H * S + 2 * H * N * M_OUT)
+
+F32 = mybir.dt.float32
+BF16 = mybir.dt.bfloat16
+I32 = mybir.dt.int32
+U32 = mybir.dt.uint32
+U16 = mybir.dt.uint16
+U8 = mybir.dt.uint8
+E4M3 = mybir.dt.float8_e4m3fn_x4
+E2M1 = mybir.dt.float4_e2m1fn_x4
+ACT = mybir.ActivationFunctionType
+ALU = mybir.AluOpType
+AX = mybir.AxisListType
+
+P = 128
+PACK = 4
+KP = P * PACK
+HALF = M_OUT // 2
+
+
+def tile_list_trail_erosion_closure_kernel(
+    tc, tab_words, tab_scales, offs, offs2, offs3, w1_words, w1_scales, w2,
+    slope, page0, wgs, gain, w3, w4_words, w4_scales, out_0, out_1, out_2,
+):
+    nc = tc.nc
+    with ExitStack() as ctx:
+        lists = ctx.enter_context(tc.tile_pool(name="lists", bufs=1))
+        keep = ctx.enter_context(tc.tile_pool(name="keep", bufs=1))
+        ring = ctx.enter_context(tc.tile_pool(name="ring", bufs=2))
+        psum = ctx.enter_context(tc.psum_pool(name="psum", bufs=1))
+
+        idx1 = lists.tile([P, S // 16], U16, name="idx1")
+        idx2 = lists.tile([P, S // 16], U16, name="idx2")
+        idx3 = lists.tile([P, M_OUT // 16], U16, name="idx3")
+
+        def held(shape, dtype, name, tag=None):
+            return keep.tile(shape, dtype, name=name, tag=tag or name, align_bytes=64)
+
+        tab_w = [held([P, T], U32, f"tab_w{a}") for a in range(2)]
+        tab_s = held([P, 2, T], U8, "tab_s")
+        w1s_raw = held([P, 2, H], U8, "w1s_raw")
+        w4s_raw = held([P, N], U8, "w4s_raw")
+        w1_raw = [held([P, 2, 2 * KP], U8, f"w1_raw{b}") for b in range(2)]
+        w4_raw = held([P, 2, N], U32, "w4_raw")
+        w2_raw = [[held([P, PACK, KP], F32, f"w2_raw{b}{a}") for a in range(2)] for b in range(2)]
+        w3_raw = [held([P, PACK, N], F32, f"w3_raw{b}") for b in range(2)]
+        slope_t = [held([P, S], F32, f"slope{i}") for i in range(8)]
+        page = [held([P, T2], F32, f"page{i}") for i in range(8)]
+        wg0 = held([P, 1, S], F32, "wg0")
+        wg1 = held([P, 1, S], F32, "wg1")
+        wg23 = held([P, 2, S], F32, "wg23")
+        wg = [wg0[:, 0, :], wg1[:, 0, :], wg23[:, 0, :], wg23[:, 1, :]]
+        gain_t = held([P, 2, PACK], F32, "gain_t")
+
+        nc.vector.memset(tab_s[:].rearrange("p a n -> p (a n)").bitcast(I32), 0)
+        nc.vector.memset(w1s_raw[:].rearrange("p a n -> p (a n)").bitcast(I32), 0)
+        nc.vector.memset(w4s_raw[:].bitcast(I32), 0)
+
+        def load_w2(b, a):
+            src = w2[KP * a : KP * (a + 1), KP * b : KP * (b + 1)].rearrange("(p j) c -> p j c", j=PACK)
+            nc.sync.dma_start(out=w2_raw[b][a][:], in_=src)
+
+        def load_w3(b):
+            src = w3[KP * b : KP * (b + 1), :].rearrange("(p j) c -> p j c", j=PACK)
+            nc.sync.dma_start(out=w3_raw[b][:], in_=src)
+
+        def load_tab(a):
+            src = tab_words[a].rearrange("p n i -> p (n i)").bitcast(I32)
+            nc.sync.dma_start(out=tab_w[a][:].bitcast(I32), in_=src)
+
+        def load_scale_rows(dst, src):
+            for q in range(4):
+                rows = src[:, 4 * q : 4 * q + 4, :].rearrange("a r n -> r a n").bitcast(I32)
+                nc.sync.dma_start(out=dst[32 * q : 32 * q + 4, :, :].bitcast(I32), in_=rows)
+
+        def load_w1(b):
+            src = w1_words[:, :, 2 * KP * b : 2 * KP * (b + 1)].rearrange("a p c -> p a c").bitcast(I32)
+            nc.sync.dma_start(out=w1_raw[b][:].bitcast(I32), in_=src)
+
+        def load_wg(dst, t0, t1):
+            src = wgs.rearrange("(q t) j -> q t j", t=PACK)[:, t0:t1, :]
+            for q in range(4):
+                nc.sync.dma_start(out=dst[32 * q : 32 * (q + 1), :, :], in_=src)
+
+        def rows_of(mat, i):
+            b, t = divmod(i, PACK)
+            return mat[KP * b : KP * (b + 1), :].rearrange("(p t) c -> p t c", t=PACK)[:, t, :]
+
+        def load_rows(i):
+            nc.sync.dma_start(out=page[i][:], in_=rows_of(page0, i))
+            if i + 1 < 8:
+                nc.sync.dma_start(out=slope_t[i + 1][:], in_=rows_of(slope, i + 1))
+
+        nc.sync.dma_start(idx1[:], offs)
+        load_w1(0)
+        nc.sync.dma_start(idx2[:], offs2)
+        load_scale_rows(tab_s, tab_scales)
+        load_w2(0, 0)
+        load_scale_rows(w1s_raw, w1_scales)
+        load_w2(0, 1)
+        load_tab(0)
+        load_tab(1)
+        nc.sync.dma_start(out=slope_t[0][:], in_=rows_of(slope, 0))
+        load_wg(wg0, 0, 1)
+        load_rows(0)
+        nc.sync.dma_start(idx3[:], offs3)
+        nc.sync.dma_start(out=gain_t[:], in_=gain.rearrange("(b p t) -> p b t", b=2, t=PACK))
+        load_w2(1, 0)
+        load_wg(wg1, 1, 2)
+        load_rows(1)
+        load_w2(1, 1)
+        load_w1(1)
+        load_wg(wg23, 2, 4)
+        load_rows(2)
+        load_w3(0)
+        load_rows(3)
+        load_w3(1)
+        nc.sync.dma_start(
+            out=w4_raw[:].bitcast(I32),
+            in_=w4_words.rearrange("a p c i -> p a (c i)").bitcast(I32),
+        )
+        for q in range(4):
+            nc.sync.dma_start(
+                out=w4s_raw[32 * q : 32 * q + 8, :].bitcast(I32),
+                in_=w4_scales[:, 4 * q : 4 * q + 4, :].bitcast(I32),
+            )
+        for i in range(4, 8):
+            load_rows(i)
+
+        def round_weight(raw, sign, name):
+            rounded = ring.tile([P, PACK * KP], BF16, name=f"{name}_bf", tag="w_bf", align_bytes=64)
+            nc.scalar.activation(
+                out=rounded[:].rearrange("p (t q j) -> p q j t", t=PACK, j=PACK),
+                in_=raw[:].rearrange("p j (q t) -> p q j t", t=PACK),
+                func=ACT.Copy,
+                scale=sign,
+            )
+            return rounded
+
+        def quantise(rounded, name, tag=None):
+            codes = held([P, KP], U32, f"{name}_codes", tag=tag)
+            scales = held([P, KP], U8, f"{name}_scales")
+            nc.vector.quantize_mx(out=codes[:].bitcast(E4M3), scales=scales[:], in_=rounded[:])
+            return codes, scales
+
+        def deal_w1_words(b):
+            dealt = held([P, 2, 2 * KP], U8, f"w1_dealt{b}")
+            nc.scalar.copy(
+                out=dealt[:].bitcast(U16).rearrange("p a (t q) -> p a t q", t=PACK),
+                in_=w1_raw[b][:].bitcast(U16).rearrange("p a (q t) -> p a t q", t=PACK),
+            )
+            return dealt
+
+        w2q = [[None, None], [None, None]]
+        w1d = [None, None]
+        v_w = [held([P, S], U32, f"v_w{a}") for a in range(2)]
+        v_s = [held([P, S], U8, f"v_s{a}") for a in range(2)]
+        w1s = held([P, 2, H], U8, "w1s")
+
+        for a in range(2):
+            nc.vector.tensor_copy(v_s[a][:], tab_s[:, a, :].indirect(idx1[:]))
+        w1d[0] = deal_w1_words(0)
+        nc.vector.tensor_copy(
+            out=w1s[:].rearrange("p a (b t q) -> p (a b) t q", b=2, t=PACK),
+            in_=w1s_raw[:].rearrange("p a (b q t) -> p (a b) t q", b=2, t=PACK),
+        )
+        for a in range(2):
+            w2q[0][a] = quantise(round_weight(w2_raw[0][a], -1.0, f"w2_0{a}"), f"w2_0{a}")
+        for a in range(2):
+            nc.vector.tensor_copy(v_w[a][:], tab_w[a][:].indirect(idx1[:]))
+
+        neg_top = held([P, 8], F32, "neg_top")
+        x_rows = [held([P, PACK, M_OUT], BF16, f"x_rows{b}") for b in range(2)]
+
+        def make_h(i):
+            b, t = divmod(i, PACK)
+            acc = psum.tile([P, S], F32, name=f"acc{i}", tag=f"bank{6 + i % 2}")
+            for a in range(2):
+                nc.tensor.matmul_mx(
+                    out=acc[:],
+                    lhsT=w1d[b][:, a, 2 * P * t : 2 * P * (t + 1)].bitcast(E2M1),
+                    lhsT_scale=w1s[:, a, KP * b + P * t : KP * b + P * (t + 1)],
+                    rhs=v_w[a][:].bitcast(E4M3),
+                    rhs_scale=v_s[a][:],
+                    start=(a == 0),
+                    stop=False,
+                )
+                codes, scales = w2q[b][a]
+                nc.tensor.matmul_mx(
+                    out=acc[:],
+                    lhsT=codes[:, P * t : P * (t + 1)].bitcast(E4M3),
+                    lhsT_scale=scales[:, P * t : P * (t + 1)],
+                    rhs=v_w[a][:].bitcast(E4M3),
+                    rhs_scale=v_s[a][:],
+                    start=False,
+                    stop=(a == 1),
+                )
+            nc.vector.tensor_tensor(slope_t[i][:], acc[:], slope_t[i][:], ALU.mult)
+
+        def scatter(i):
+            nc.vector.tensor_tensor(page[i][:].indirect(idx2[:]), slope_t[i][:], wg[i % PACK], ALU.mult)
+
+        def row_max(i):
+            nc.vector.tensor_reduce(neg_top[:, i : i + 1], page[i][:], AX.X, ALU.max, negate=True)
+
+        def look(i, m0, m1):
+            b, t = divmod(i, PACK)
+            looked = ring.tile([P, m1 - m0], F32, name=f"look{i}_{m0}", tag="look")
+            nc.scalar.activation(
+                out=looked[:],
+                in_=page[i][:].indirect(idx3[:, m0 // 16 : m1 // 16]),
+                func=ACT.Exp,
+                bias=neg_top[:, i : i + 1],
+            )
+            nc.scalar.activation(
+                out=x_rows[b][:, t, m0:m1], in_=looked[:], func=ACT.Copy, scale=gain_t[:, b, t : t + 1]
+            )
+
+        def weave(copy, dst, src):
+            copy(
+                out=dst[:].rearrange("p (c i t) -> p c t i", t=PACK, i=4),
+                in_=src.rearrange("p t (c i) -> p c t i", i=4),
+            )
+
+        make_h(0)
+        scatter(0)
+        make_h(1)
+        row_max(0)
+        look(0, 0, M_OUT)
+        w2_10 = round_weight(w2_raw[1][0], -1.0, "w2_10")
+        scatter(1)
+        make_h(2)
+        row_max(1)
+        look(1, 0, M_OUT)
+        w2q[1][0] = quantise(w2_10, "w2_10", tag="slope1")
+        w2_11 = round_weight(w2_raw[1][1], -1.0, "w2_11")
+        w1d[1] = deal_w1_words(1)
+        scatter(2)
+        make_h(3)
+        row_max(2)
+        look(2, 0, M_OUT)
+        w2q[1][1] = quantise(w2_11, "w2_11", tag="slope2")
+        w3_0 = round_weight(w3_raw[0], 1.0, "w3_0")
+        scatter(3)
+        make_h(4)
+        row_max(3)
+        look(3, 0, M_OUT)
+        w3_1 = round_weight(w3_raw[1], 1.0, "w3_1")
+        w4d = held([P, 2, N], U32, "w4d")
+        nc.scalar.copy(
+            out=w4d[:].rearrange("p a (t q) -> p a t q", t=PACK),
+            in_=w4_raw[:].rearrange("p a (q t) -> p a t q", t=PACK),
+        )
+        w4s = held([P, N], U8, "w4s")
+        nc.vector.tensor_copy(
+            out=w4s[:].rearrange("p (t q) -> p t q", t=PACK),
+            in_=w4s_raw[:].rearrange("p (q t) -> p t q", t=PACK),
+        )
+        x0_bf = held([P, PACK * M_OUT], BF16, "x0_bf")
+        weave(nc.scalar.copy, x0_bf, x_rows[0][:])
+        scatter(4)
+        make_h(5)
+        row_max(4)
+        look(4, 0, M_OUT)
+        w3q = [quantise(w3_0, "w3_0", tag="slope4")]
+        scatter(5)
+        make_h(6)
+        row_max(5)
+        look(5, 0, M_OUT)
+        w3q.append(quantise(w3_1, "w3_1", tag="slope5"))
+        scatter(6)
+        make_h(7)
+        row_max(6)
+        look(6, 0, M_OUT)
+        scatter(7)
+        x0_codes = held([P, M_OUT], U32, "x0_codes", tag="slope7")
+        x0_scales = held([P, M_OUT], U8, "x0_scales")
+
+        def quantise_x0(hf):
+            cols = slice(HALF * hf, HALF * (hf + 1))
+            nc.vector.quantize_mx(
+                out=x0_codes[:, cols].bitcast(E4M3),
+                scales=x0_scales[:, cols],
+                in_=x0_bf[:, PACK * HALF * hf : PACK * HALF * (hf + 1)],
+            )
+
+        quantise_x0(0)
+        row_max(7)
+        quantise_x0(1)
+
+        banks = {}
+
+        def second_stage(b, hf, x_codes, x_scales):
+            for u in range(2):
+                for w in range(2):
+                    if b == 0:
+                        banks[hf, u, w] = psum.tile(
+                            [P, 2, HALF], F32, name=f"y{hf}{u}{w}", tag=f"bank{4 * hf + 2 * u + w}"
+                        )
+                    for e in range(2):
+                        cols = slice(P * (2 * u + e), P * (2 * u + e + 1))
+                        if w == 0:
+                            codes, scales = w3q[b][0][:, cols], w3q[b][1][:, cols]
+                        else:
+                            codes, scales = w4d[:, b, cols], w4s[4 * b : P, cols]
+                        nc.tensor.matmul_mx(
+                            out=banks[hf, u, w][:, e, :],
+                            lhsT=codes.bitcast(E4M3),
+                            lhsT_scale=scales,
+                            rhs=x_codes.bitcast(E4M3),
+                            rhs_scale=x_scales,
+                            start=(b == 0 and e == 0),
+                            stop=(b == 1 and e == 1),
+                        )
+
+        for hf in range(2):
+            cols = slice(HALF * hf, HALF * (hf + 1))
+            second_stage(0, hf, x0_codes[:, cols], x0_scales[:, cols])
+
+        y_scales = held([P, M_OUT], U8, "y_scales")
+        for hf in range(2):
+            look(7, HALF * hf, HALF * (hf + 1))
+        for hf in range(2):
+            cols = slice(HALF * hf, HALF * (hf + 1))
+            x1_bf = held([P, PACK * HALF], BF16, f"x1_bf{hf}")
+            weave(nc.vector.tensor_copy, x1_bf, x_rows[1][:, :, cols])
+            x1_codes = held([P, HALF], U32, f"x1_codes{hf}")
+            x1_scales = held([P, HALF], U8, f"x1_scales{hf}")
+            nc.vector.quantize_mx(out=x1_codes[:].bitcast(E4M3), scales=x1_scales[:], in_=x1_bf[:])
+            second_stage(1, hf, x1_codes[:], x1_scales[:])
+        for hf in range(2):
+            cols = slice(HALF * hf, HALF * (hf + 1))
+            y = held([P, PACK, HALF], F32, f"y{hf}")
+            for u in range(2):
+                y3 = ring.tile([P, 2, HALF], F32, name=f"y3_{hf}{u}", tag="y3")
+                nc.scalar.copy(out=y3[:], in_=banks[hf, u, 0][:])
+                nc.vector.tensor_tensor(y[:, 2 * u : 2 * u + 2, :], banks[hf, u, 1][:], y3[:], ALU.mult)
+            nc.sync.dma_start(out=out_0.rearrange("(p t) m -> p t m", t=PACK)[:, :, cols], in_=y[:])
+            y_bf = held([P, PACK * HALF], BF16, f"y_bf{hf}")
+            weave(nc.vector.tensor_copy, y_bf, y[:])
+            y_codes = held([P, HALF], U32, f"y_codes{hf}")
+            nc.vector.quantize_mx(out=y_codes[:].bitcast(E4M3), scales=y_scales[:, cols], in_=y_bf[:])
+            nc.sync.dma_start(
+                out=out_1[0].rearrange("p m i -> p (m i)").bitcast(I32)[:, cols], in_=y_codes[:].bitcast(I32)
+            )
+        for q in range(4):
+            queue = nc.scalar if q % 2 else nc.sync
+            queue.dma_start(
+                out=out_2[0, 4 * q : 4 * q + 4, :].bitcast(I32), in_=y_scales[32 * q : 32 * q + 4, :].bitcast(I32)
+            )

@@ -20,7 +20,11 @@ AX = mybir.AxisListType
 P = 128
 PACK = 4
 KP = P * PACK
-HALF = M_OUT // 2
+TILES = H // P
+LAST = TILES - 1
+WHOLE = slice(0, 512)
+HALVES = (slice(0, 256), slice(256, 512))
+HALF = 256
 
 
 def tile_list_trail_erosion_closure_kernel(
@@ -38,6 +42,9 @@ def tile_list_trail_erosion_closure_kernel(
         idx2 = lists.tile([P, S // 16], U16, name="idx2")
         idx3 = lists.tile([P, M_OUT // 16], U16, name="idx3")
 
+        def entries(idx, cols):
+            return idx[:, cols.start // 16 : cols.stop // 16]
+
         def held(shape, dtype, name, tag=None):
             return keep.tile(shape, dtype, name=name, tag=tag or name, align_bytes=64)
 
@@ -49,8 +56,8 @@ def tile_list_trail_erosion_closure_kernel(
         w4_raw = held([P, 2, N], U32, "w4_raw")
         w2_raw = [[held([P, PACK, KP], F32, f"w2_raw{b}{a}") for a in range(2)] for b in range(2)]
         w3_raw = [held([P, PACK, N], F32, f"w3_raw{b}") for b in range(2)]
-        slope_t = [held([P, S], F32, f"slope{i}") for i in range(8)]
-        page = [held([P, T2], F32, f"page{i}") for i in range(8)]
+        h = [held([P, S], F32, f"h{i}") for i in range(TILES)]
+        page = [held([P, T2], F32, f"page{i}") for i in range(TILES)]
         wg0 = held([P, 1, S], F32, "wg0")
         wg1 = held([P, 1, S], F32, "wg1")
         wg23 = held([P, 2, S], F32, "wg23")
@@ -73,10 +80,10 @@ def tile_list_trail_erosion_closure_kernel(
             src = tab_words[a].rearrange("p n i -> p (n i)").bitcast(I32)
             nc.sync.dma_start(out=tab_w[a][:].bitcast(I32), in_=src)
 
-        def load_scale_rows(dst, src):
+        def load_scale_rows(queue, dst, src):
             for q in range(4):
                 rows = src[:, 4 * q : 4 * q + 4, :].rearrange("a r n -> r a n").bitcast(I32)
-                nc.sync.dma_start(out=dst[32 * q : 32 * q + 4, :, :].bitcast(I32), in_=rows)
+                queue.dma_start(out=dst[32 * q : 32 * q + 4, :, :].bitcast(I32), in_=rows)
 
         def load_w1(b):
             src = w1_words[:, :, 2 * KP * b : 2 * KP * (b + 1)].rearrange("a p c -> p a c").bitcast(I32)
@@ -93,24 +100,24 @@ def tile_list_trail_erosion_closure_kernel(
 
         def load_rows(i):
             nc.sync.dma_start(out=page[i][:], in_=rows_of(page0, i))
-            if i + 1 < 8:
-                nc.sync.dma_start(out=slope_t[i + 1][:], in_=rows_of(slope, i + 1))
+            if i < LAST:
+                nc.sync.dma_start(out=h[i + 1][:], in_=rows_of(slope, i + 1))
 
+        load_scale_rows(nc.gpsimd, w1s_raw, w1_scales)
         nc.sync.dma_start(idx1[:], offs)
-        load_w1(0)
-        nc.sync.dma_start(idx2[:], offs2)
-        load_scale_rows(tab_s, tab_scales)
         load_w2(0, 0)
-        load_scale_rows(w1s_raw, w1_scales)
+        load_scale_rows(nc.sync, tab_s, tab_scales)
         load_w2(0, 1)
+        load_w1(0)
         load_tab(0)
         load_tab(1)
-        nc.sync.dma_start(out=slope_t[0][:], in_=rows_of(slope, 0))
+        nc.sync.dma_start(out=h[0][:], in_=rows_of(slope, 0))
+        nc.sync.dma_start(idx2[:], offs2)
         load_wg(wg0, 0, 1)
         load_rows(0)
+        load_w2(1, 0)
         nc.sync.dma_start(idx3[:], offs3)
         nc.sync.dma_start(out=gain_t[:], in_=gain.rearrange("(b p t) -> p b t", b=2, t=PACK))
-        load_w2(1, 0)
         load_wg(wg1, 1, 2)
         load_rows(1)
         load_w2(1, 1)
@@ -129,7 +136,7 @@ def tile_list_trail_erosion_closure_kernel(
                 out=w4s_raw[32 * q : 32 * q + 8, :].bitcast(I32),
                 in_=w4_scales[:, 4 * q : 4 * q + 4, :].bitcast(I32),
             )
-        for i in range(4, 8):
+        for i in range(4, TILES):
             load_rows(i)
 
         def round_weight(raw, sign, name):
@@ -143,50 +150,52 @@ def tile_list_trail_erosion_closure_kernel(
             return rounded
 
         def quantise(rounded, name, tag=None):
-            codes = held([P, KP], U32, f"{name}_codes", tag=tag)
-            scales = held([P, KP], U8, f"{name}_scales")
+            width = rounded.shape[1] // PACK
+            codes = held([P, width], U32, f"{name}_codes", tag=tag)
+            scales = held([P, width], U8, f"{name}_scales")
             nc.vector.quantize_mx(out=codes[:].bitcast(E4M3), scales=scales[:], in_=rounded[:])
             return codes, scales
 
+        def deal(copy, dst, src):
+            copy(out=dst.rearrange("p a (t q) -> p a q t", t=PACK), in_=src.rearrange("p a (q t) -> p a q t", t=PACK))
+
         def deal_w1_words(b):
             dealt = held([P, 2, 2 * KP], U8, f"w1_dealt{b}")
-            nc.scalar.copy(
-                out=dealt[:].bitcast(U16).rearrange("p a (t q) -> p a t q", t=PACK),
-                in_=w1_raw[b][:].bitcast(U16).rearrange("p a (q t) -> p a t q", t=PACK),
-            )
+            deal(nc.scalar.copy, dealt[:].bitcast(U16), w1_raw[b][:].bitcast(U16))
             return dealt
 
         w2q = [[None, None], [None, None]]
         w1d = [None, None]
         v_w = [held([P, S], U32, f"v_w{a}") for a in range(2)]
         v_s = [held([P, S], U8, f"v_s{a}") for a in range(2)]
-        w1s = held([P, 2, H], U8, "w1s")
 
         for a in range(2):
             nc.vector.tensor_copy(v_s[a][:], tab_s[:, a, :].indirect(idx1[:]))
-        w1d[0] = deal_w1_words(0)
+        w1s = held([P, 2, H], U8, "w1s", tag="tab_s")
         nc.vector.tensor_copy(
             out=w1s[:].rearrange("p a (b t q) -> p (a b) t q", b=2, t=PACK),
             in_=w1s_raw[:].rearrange("p a (b q t) -> p (a b) t q", b=2, t=PACK),
         )
         for a in range(2):
             w2q[0][a] = quantise(round_weight(w2_raw[0][a], -1.0, f"w2_0{a}"), f"w2_0{a}")
-        for a in range(2):
-            nc.vector.tensor_copy(v_w[a][:], tab_w[a][:].indirect(idx1[:]))
+        w1d[0] = deal_w1_words(0)
+        nc.vector.tensor_copy(v_w[0][:], tab_w[0][:].indirect(idx1[:]))
+        for cols in HALVES:
+            nc.vector.tensor_copy(v_w[1][:, cols], tab_w[1][:].indirect(entries(idx1, cols)))
 
-        neg_top = held([P, 8], F32, "neg_top")
-        x_rows = [held([P, PACK, M_OUT], BF16, f"x_rows{b}") for b in range(2)]
+        neg_top = held([P, TILES], F32, "neg_top")
+        x_rows = [held([P, PACK - b, M_OUT], BF16, f"x_rows{b}") for b in range(2)]
 
-        def make_h(i):
+        def make_h(i, cols, bank):
             b, t = divmod(i, PACK)
-            acc = psum.tile([P, S], F32, name=f"acc{i}", tag=f"bank{6 + i % 2}")
+            acc = psum.tile([P, cols.stop - cols.start], F32, name=f"acc{i}_{cols.start}", tag=f"bank{bank}")
             for a in range(2):
                 nc.tensor.matmul_mx(
                     out=acc[:],
                     lhsT=w1d[b][:, a, 2 * P * t : 2 * P * (t + 1)].bitcast(E2M1),
                     lhsT_scale=w1s[:, a, KP * b + P * t : KP * b + P * (t + 1)],
-                    rhs=v_w[a][:].bitcast(E4M3),
-                    rhs_scale=v_s[a][:],
+                    rhs=v_w[a][:, cols].bitcast(E4M3),
+                    rhs_scale=v_s[a][:, cols],
                     start=(a == 0),
                     stop=False,
                 )
@@ -195,67 +204,66 @@ def tile_list_trail_erosion_closure_kernel(
                     out=acc[:],
                     lhsT=codes[:, P * t : P * (t + 1)].bitcast(E4M3),
                     lhsT_scale=scales[:, P * t : P * (t + 1)],
-                    rhs=v_w[a][:].bitcast(E4M3),
-                    rhs_scale=v_s[a][:],
+                    rhs=v_w[a][:, cols].bitcast(E4M3),
+                    rhs_scale=v_s[a][:, cols],
                     start=False,
                     stop=(a == 1),
                 )
-            nc.vector.tensor_tensor(slope_t[i][:], acc[:], slope_t[i][:], ALU.mult)
+            nc.vector.tensor_tensor(h[i][:, cols], acc[:], h[i][:, cols], ALU.mult)
 
-        def scatter(i):
-            nc.vector.tensor_tensor(page[i][:].indirect(idx2[:]), slope_t[i][:], wg[i % PACK], ALU.mult)
+        def scatter(i, cols):
+            window = page[i][:].indirect(entries(idx2, cols))
+            nc.vector.tensor_tensor(window, h[i][:, cols], wg[i % PACK][:, cols], ALU.mult)
 
         def row_max(i):
             nc.vector.tensor_reduce(neg_top[:, i : i + 1], page[i][:], AX.X, ALU.max, negate=True)
 
-        def look(i, m0, m1):
-            b, t = divmod(i, PACK)
-            looked = ring.tile([P, m1 - m0], F32, name=f"look{i}_{m0}", tag="look")
+        def look(i, cols, tag):
+            looked = held([P, cols.stop - cols.start], F32, f"look{i}_{cols.start}", tag=tag)
             nc.scalar.activation(
                 out=looked[:],
-                in_=page[i][:].indirect(idx3[:, m0 // 16 : m1 // 16]),
+                in_=page[i][:].indirect(entries(idx3, cols)),
                 func=ACT.Exp,
                 bias=neg_top[:, i : i + 1],
             )
-            nc.scalar.activation(
-                out=x_rows[b][:, t, m0:m1], in_=looked[:], func=ACT.Copy, scale=gain_t[:, b, t : t + 1]
-            )
+            return looked
+
+        def look_row(i, tag):
+            b, t = divmod(i, PACK)
+            looked = look(i, WHOLE, tag)
+            nc.scalar.activation(out=x_rows[b][:, t, :], in_=looked[:], func=ACT.Copy, scale=gain_t[:, b, t : t + 1])
 
         def weave(copy, dst, src):
+            slots = src.shape[1]
             copy(
-                out=dst[:].rearrange("p (c i t) -> p c t i", t=PACK, i=4),
+                out=dst[:].rearrange("p (c i t) -> p c t i", t=PACK, i=4)[:, :, 0:slots, :],
                 in_=src.rearrange("p t (c i) -> p c t i", i=4),
             )
 
-        make_h(0)
-        scatter(0)
-        make_h(1)
+        def step(i, tag):
+            scatter(i, WHOLE)
+            make_h(i + 1, WHOLE, 6 + i % 2)
+            row_max(i)
+            look_row(i, tag)
+
+        for half, cols in enumerate(HALVES):
+            make_h(0, cols, half)
+            scatter(0, cols)
+        make_h(1, WHOLE, 6)
         row_max(0)
-        look(0, 0, M_OUT)
         w2_10 = round_weight(w2_raw[1][0], -1.0, "w2_10")
-        scatter(1)
-        make_h(2)
-        row_max(1)
-        look(1, 0, M_OUT)
-        w2q[1][0] = quantise(w2_10, "w2_10", tag="slope1")
+        look_row(0, "w2_raw10")
         w2_11 = round_weight(w2_raw[1][1], -1.0, "w2_11")
         w1d[1] = deal_w1_words(1)
-        scatter(2)
-        make_h(3)
-        row_max(2)
-        look(2, 0, M_OUT)
-        w2q[1][1] = quantise(w2_11, "w2_11", tag="slope2")
+        step(1, "w2_raw11")
+        w2q[1][0] = quantise(w2_10, "w2_10", tag="h1")
         w3_0 = round_weight(w3_raw[0], 1.0, "w3_0")
-        scatter(3)
-        make_h(4)
-        row_max(3)
-        look(3, 0, M_OUT)
+        step(2, "w3_raw0")
+        w2q[1][1] = quantise(w2_11, "w2_11", tag="h2")
         w3_1 = round_weight(w3_raw[1], 1.0, "w3_1")
+        step(3, "w3_raw1")
         w4d = held([P, 2, N], U32, "w4d")
-        nc.scalar.copy(
-            out=w4d[:].rearrange("p a (t q) -> p a t q", t=PACK),
-            in_=w4_raw[:].rearrange("p a (q t) -> p a t q", t=PACK),
-        )
+        deal(nc.scalar.copy, w4d[:], w4_raw[:])
         w4s = held([P, N], U8, "w4s")
         nc.vector.tensor_copy(
             out=w4s[:].rearrange("p (t q) -> p t q", t=PACK),
@@ -263,44 +271,37 @@ def tile_list_trail_erosion_closure_kernel(
         )
         x0_bf = held([P, PACK * M_OUT], BF16, "x0_bf")
         weave(nc.scalar.copy, x0_bf, x_rows[0][:])
-        scatter(4)
-        make_h(5)
-        row_max(4)
-        look(4, 0, M_OUT)
-        w3q = [quantise(w3_0, "w3_0", tag="slope4")]
-        scatter(5)
-        make_h(6)
-        row_max(5)
-        look(5, 0, M_OUT)
-        w3q.append(quantise(w3_1, "w3_1", tag="slope5"))
-        scatter(6)
-        make_h(7)
-        row_max(6)
-        look(6, 0, M_OUT)
-        scatter(7)
-        x0_codes = held([P, M_OUT], U32, "x0_codes", tag="slope7")
+        step(4, "w2_raw10")
+        w3q = [quantise(w3_0, "w3_0", tag="h4")]
+        step(5, "w2_raw11")
+        w3q.append(quantise(w3_1, "w3_1", tag="h5"))
+        step(6, "w3_raw0")
+        x1_bf = [held([P, PACK * HALF], BF16, f"x1_bf{half}") for half in range(2)]
+        for half, cols in enumerate(HALVES):
+            weave(nc.scalar.copy, x1_bf[half], x_rows[1][:, :, cols])
+        scatter(LAST, WHOLE)
+        x0_codes = held([P, M_OUT], U32, "x0_codes", tag=f"h{LAST}")
         x0_scales = held([P, M_OUT], U8, "x0_scales")
 
-        def quantise_x0(hf):
-            cols = slice(HALF * hf, HALF * (hf + 1))
+        def quantise_x0(cols):
             nc.vector.quantize_mx(
                 out=x0_codes[:, cols].bitcast(E4M3),
                 scales=x0_scales[:, cols],
-                in_=x0_bf[:, PACK * HALF * hf : PACK * HALF * (hf + 1)],
+                in_=x0_bf[:, PACK * cols.start : PACK * cols.stop],
             )
 
-        quantise_x0(0)
-        row_max(7)
-        quantise_x0(1)
+        quantise_x0(HALVES[0])
+        row_max(LAST)
+        quantise_x0(HALVES[1])
 
         banks = {}
 
-        def second_stage(b, hf, x_codes, x_scales):
+        def second_stage(b, half, x_codes, x_scales):
             for u in range(2):
                 for w in range(2):
                     if b == 0:
-                        banks[hf, u, w] = psum.tile(
-                            [P, 2, HALF], F32, name=f"y{hf}{u}{w}", tag=f"bank{4 * hf + 2 * u + w}"
+                        banks[half, u, w] = psum.tile(
+                            [P, 2, HALF], F32, name=f"y{half}{u}{w}", tag=f"bank{4 * half + 2 * u + w}"
                         )
                     for e in range(2):
                         cols = slice(P * (2 * u + e), P * (2 * u + e + 1))
@@ -309,7 +310,7 @@ def tile_list_trail_erosion_closure_kernel(
                         else:
                             codes, scales = w4d[:, b, cols], w4s[4 * b : P, cols]
                         nc.tensor.matmul_mx(
-                            out=banks[hf, u, w][:, e, :],
+                            out=banks[half, u, w][:, e, :],
                             lhsT=codes.bitcast(E4M3),
                             lhsT_scale=scales,
                             rhs=x_codes.bitcast(E4M3),
@@ -318,33 +319,35 @@ def tile_list_trail_erosion_closure_kernel(
                             stop=(b == 1 and e == 1),
                         )
 
-        for hf in range(2):
-            cols = slice(HALF * hf, HALF * (hf + 1))
-            second_stage(0, hf, x0_codes[:, cols], x0_scales[:, cols])
+        for half, cols in enumerate(HALVES):
+            second_stage(0, half, x0_codes[:, cols], x0_scales[:, cols])
 
-        y_scales = held([P, M_OUT], U8, "y_scales")
-        for hf in range(2):
-            look(7, HALF * hf, HALF * (hf + 1))
-        for hf in range(2):
-            cols = slice(HALF * hf, HALF * (hf + 1))
-            x1_bf = held([P, PACK * HALF], BF16, f"x1_bf{hf}")
-            weave(nc.vector.tensor_copy, x1_bf, x_rows[1][:, :, cols])
-            x1_codes = held([P, HALF], U32, f"x1_codes{hf}")
-            x1_scales = held([P, HALF], U8, f"x1_scales{hf}")
-            nc.vector.quantize_mx(out=x1_codes[:].bitcast(E4M3), scales=x1_scales[:], in_=x1_bf[:])
-            second_stage(1, hf, x1_codes[:], x1_scales[:])
-        for hf in range(2):
-            cols = slice(HALF * hf, HALF * (hf + 1))
-            y = held([P, PACK, HALF], F32, f"y{hf}")
+        for half, cols in enumerate(HALVES):
+            looked = look(LAST, cols, None)
+            nc.vector.tensor_scalar(
+                x1_bf[half][:].rearrange("p (m t) -> p m t", t=PACK)[:, :, PACK - 1],
+                looked[:],
+                gain_t[:, 1, PACK - 1 : PACK],
+                None,
+                ALU.mult,
+            )
+            x1_codes, x1_scales = quantise(x1_bf[half], f"x1_{half}")
+            second_stage(1, half, x1_codes[:], x1_scales[:])
+
+        y = [held([P, PACK, HALF], F32, f"y{half}") for half in range(2)]
+        for half, cols in enumerate(HALVES):
             for u in range(2):
-                y3 = ring.tile([P, 2, HALF], F32, name=f"y3_{hf}{u}", tag="y3")
-                nc.scalar.copy(out=y3[:], in_=banks[hf, u, 0][:])
-                nc.vector.tensor_tensor(y[:, 2 * u : 2 * u + 2, :], banks[hf, u, 1][:], y3[:], ALU.mult)
-            nc.sync.dma_start(out=out_0.rearrange("(p t) m -> p t m", t=PACK)[:, :, cols], in_=y[:])
-            y_bf = held([P, PACK * HALF], BF16, f"y_bf{hf}")
-            weave(nc.vector.tensor_copy, y_bf, y[:])
-            y_codes = held([P, HALF], U32, f"y_codes{hf}")
-            nc.vector.quantize_mx(out=y_codes[:].bitcast(E4M3), scales=y_scales[:, cols], in_=y_bf[:])
+                y3 = ring.tile([P, 2, HALF], F32, name=f"y3_{half}{u}", tag="y3")
+                nc.scalar.copy(out=y3[:], in_=banks[half, u, 0][:])
+                nc.vector.tensor_tensor(y[half][:, 2 * u : 2 * u + 2, :], banks[half, u, 1][:], y3[:], ALU.mult)
+            nc.sync.dma_start(out=out_0.rearrange("(p t) m -> p t m", t=PACK)[:, :, cols], in_=y[half][:])
+        y_bf = [held([P, PACK * HALF], BF16, f"y_bf{half}") for half in range(2)]
+        weave(nc.scalar.copy, y_bf[0], y[0][:])
+        weave(nc.vector.tensor_copy, y_bf[1], y[1][:])
+        y_scales = held([P, M_OUT], U8, "y_scales")
+        for half, cols in enumerate(HALVES):
+            y_codes = held([P, HALF], U32, f"y_codes{half}")
+            nc.vector.quantize_mx(out=y_codes[:].bitcast(E4M3), scales=y_scales[:, cols], in_=y_bf[half][:])
             nc.sync.dma_start(
                 out=out_1[0].rearrange("p m i -> p (m i)").bitcast(I32)[:, cols], in_=y_codes[:].bitcast(I32)
             )

@@ -1,6 +1,7 @@
 from contextlib import ExitStack
 
 import concourse.mybir as mybir
+from concourse.masks import make_identity
 
 K, T, S, T2, M_OUT, H, N = 1024, 2048, 512, 1024, 512, 1024, 512
 FLOPS = 2 * (2 * K * H * S + 2 * H * N * M_OUT)
@@ -58,10 +59,10 @@ def tile_list_trail_erosion_closure_kernel(
         w3_raw = [held([P, PACK, N], F32, f"w3_raw{b}") for b in range(2)]
         h = [held([P, S], F32, f"h{i}") for i in range(TILES)]
         page = [held([P, T2], F32, f"page{i}") for i in range(TILES)]
-        wg0 = held([P, 1, S], F32, "wg0")
-        wg1 = held([P, 1, S], F32, "wg1")
-        wg23 = held([P, 2, S], F32, "wg23")
-        wg = [wg0[:, 0, :], wg1[:, 0, :], wg23[:, 0, :], wg23[:, 1, :]]
+        wgs_raw = held([P, S], F32, "wgs_raw")
+        wg = [held([P, S], F32, f"wg{t}") for t in range(PACK)]
+        ident = held([P, P], F32, "ident")
+        make_identity(nc, ident[:])
         gain_t = held([P, 2, PACK], F32, "gain_t")
 
         nc.vector.memset(tab_s[:].rearrange("p a n -> p (a n)").bitcast(I32), 0)
@@ -89,11 +90,6 @@ def tile_list_trail_erosion_closure_kernel(
             src = w1_words[:, :, 2 * KP * b : 2 * KP * (b + 1)].rearrange("a p c -> p a c").bitcast(I32)
             nc.sync.dma_start(out=w1_raw[b][:].bitcast(I32), in_=src)
 
-        def load_wg(dst, t0, t1):
-            src = wgs.rearrange("(q t) j -> q t j", t=PACK)[:, t0:t1, :]
-            for q in range(4):
-                nc.sync.dma_start(out=dst[32 * q : 32 * (q + 1), :, :], in_=src)
-
         def rows_of(mat, i):
             b, t = divmod(i, PACK)
             return mat[KP * b : KP * (b + 1), :].rearrange("(p t) c -> p t c", t=PACK)[:, t, :]
@@ -103,29 +99,28 @@ def tile_list_trail_erosion_closure_kernel(
             if i < LAST:
                 nc.sync.dma_start(out=h[i + 1][:], in_=rows_of(slope, i + 1))
 
-        load_scale_rows(nc.gpsimd, w1s_raw, w1_scales)
         nc.sync.dma_start(idx1[:], offs)
-        load_w2(0, 0)
+        nc.sync.dma_start(out=wgs_raw[:], in_=wgs)
+        nc.sync.dma_start(idx2[:], offs2)
         load_scale_rows(nc.sync, tab_s, tab_scales)
+        load_w2(0, 0)
         load_w2(0, 1)
+        load_scale_rows(nc.sync, w1s_raw, w1_scales)
         load_w1(0)
         load_tab(0)
         load_tab(1)
         nc.sync.dma_start(out=h[0][:], in_=rows_of(slope, 0))
-        nc.sync.dma_start(idx2[:], offs2)
-        load_wg(wg0, 0, 1)
         load_rows(0)
-        load_w2(1, 0)
         nc.sync.dma_start(idx3[:], offs3)
         nc.sync.dma_start(out=gain_t[:], in_=gain.rearrange("(b p t) -> p b t", b=2, t=PACK))
-        load_wg(wg1, 1, 2)
         load_rows(1)
+        load_w2(1, 0)
+        load_rows(2)
         load_w2(1, 1)
         load_w1(1)
-        load_wg(wg23, 2, 4)
-        load_rows(2)
         load_w3(0)
         load_rows(3)
+        load_rows(4)
         load_w3(1)
         nc.sync.dma_start(
             out=w4_raw[:].bitcast(I32),
@@ -136,8 +131,23 @@ def tile_list_trail_erosion_closure_kernel(
                 out=w4s_raw[32 * q : 32 * q + 8, :].bitcast(I32),
                 in_=w4_scales[:, 4 * q : 4 * q + 4, :].bitcast(I32),
             )
-        for i in range(4, TILES):
+        for i in range(5, TILES):
             load_rows(i)
+
+        wgs_turned = psum.tile([P, S // P, P], F32, name="wgs_turned", tag="bank2")
+        for c in range(S // P):
+            nc.tensor.transpose(wgs_turned[:, c, :], wgs_raw[:, P * c : P * (c + 1)], ident[:])
+
+        def spread_wg(t, tag):
+            rows = wgs_turned[:].rearrange("p c (q t) -> p c t q", t=PACK)[:, :, t : t + 1, :]
+            repeated = held([P, S // P, 4, 32], F32, f"wg_rep{t}", tag=tag)
+            nc.scalar.copy(out=repeated[:], in_=rows.to_broadcast([P, S // P, 4, 32]))
+            back = psum.tile([P, S // P, P], F32, name=f"wg_back{t}", tag=f"bank{3 + t % 2}")
+            for c in range(S // P):
+                nc.tensor.transpose(back[:, c, :], repeated[:, c, :, :].rearrange("p r q -> p (r q)"), ident[:])
+            nc.scalar.copy(out=wg[t][:], in_=back[:].rearrange("p c j -> p (c j)"))
+
+        spread_wg(0, None)
 
         def round_weight(raw, sign, name):
             rounded = ring.tile([P, PACK * KP], BF16, name=f"{name}_bf", tag="w_bf", align_bytes=64)
@@ -171,7 +181,7 @@ def tile_list_trail_erosion_closure_kernel(
 
         for a in range(2):
             nc.vector.tensor_copy(v_s[a][:], tab_s[:, a, :].indirect(idx1[:]))
-        w1s = held([P, 2, H], U8, "w1s", tag="tab_s")
+        w1s = held([P, 2, H], U8, "w1s")
         nc.vector.tensor_copy(
             out=w1s[:].rearrange("p a (b t q) -> p (a b) t q", b=2, t=PACK),
             in_=w1s_raw[:].rearrange("p a (b q t) -> p (a b) t q", b=2, t=PACK),
@@ -247,21 +257,23 @@ def tile_list_trail_erosion_closure_kernel(
             look_row(i, tag)
 
         for half, cols in enumerate(HALVES):
-            make_h(0, cols, half)
+            make_h(0, cols, 6 + half)
             scatter(0, cols)
         make_h(1, WHOLE, 6)
+        for t in range(1, PACK):
+            spread_wg(t, "tab_w1")
         row_max(0)
+        look_row(0, None)
         w2_10 = round_weight(w2_raw[1][0], -1.0, "w2_10")
-        look_row(0, "w2_raw10")
+        step(1, "w2_raw10")
         w2_11 = round_weight(w2_raw[1][1], -1.0, "w2_11")
         w1d[1] = deal_w1_words(1)
-        step(1, "w2_raw11")
+        step(2, "w2_raw11")
         w2q[1][0] = quantise(w2_10, "w2_10", tag="h1")
-        w3_0 = round_weight(w3_raw[0], 1.0, "w3_0")
-        step(2, "w3_raw0")
         w2q[1][1] = quantise(w2_11, "w2_11", tag="h2")
+        w3_0 = round_weight(w3_raw[0], 1.0, "w3_0")
+        step(3, "w3_raw0")
         w3_1 = round_weight(w3_raw[1], 1.0, "w3_1")
-        step(3, "w3_raw1")
         w4d = held([P, 2, N], U32, "w4d")
         deal(nc.scalar.copy, w4d[:], w4_raw[:])
         w4s = held([P, N], U8, "w4s")
@@ -271,11 +283,11 @@ def tile_list_trail_erosion_closure_kernel(
         )
         x0_bf = held([P, PACK * M_OUT], BF16, "x0_bf")
         weave(nc.scalar.copy, x0_bf, x_rows[0][:])
-        step(4, "w2_raw10")
+        step(4, "w3_raw1")
         w3q = [quantise(w3_0, "w3_0", tag="h4")]
-        step(5, "w2_raw11")
+        step(5, "w2_raw10")
         w3q.append(quantise(w3_1, "w3_1", tag="h5"))
-        step(6, "w3_raw0")
+        step(6, "w2_raw11")
         x1_bf = [held([P, PACK * HALF], BF16, f"x1_bf{half}") for half in range(2)]
         for half, cols in enumerate(HALVES):
             weave(nc.scalar.copy, x1_bf[half], x_rows[1][:, :, cols])

@@ -21,11 +21,18 @@ AX = mybir.AxisListType
 P = 128
 PACK = 4
 KP = P * PACK
+PASSES = 2
+QUADS, QUAD = 4, 32
+PER_COLUMN = 16
+RUN = 4
 TILES = H // P
 LAST = TILES - 1
-WHOLE = slice(0, 512)
-HALVES = (slice(0, 256), slice(256, 512))
 HALF = 256
+WHOLE = slice(0, 2 * HALF)
+HALVES = (slice(0, HALF), slice(HALF, 2 * HALF))
+FIRST_STAGE_BANKS = (6, 7)
+TURNED_BANK = 2
+BACK_BANKS = (3, 4)
 
 
 def tile_list_trail_erosion_closure_kernel(
@@ -39,60 +46,60 @@ def tile_list_trail_erosion_closure_kernel(
         ring = ctx.enter_context(tc.tile_pool(name="ring", bufs=2))
         psum = ctx.enter_context(tc.psum_pool(name="psum", bufs=1))
 
-        idx1 = lists.tile([P, S // 16], U16, name="idx1")
-        idx2 = lists.tile([P, S // 16], U16, name="idx2")
-        idx3 = lists.tile([P, M_OUT // 16], U16, name="idx3")
+        idx1 = lists.tile([P, S // PER_COLUMN], U16, name="idx1")
+        idx2 = lists.tile([P, S // PER_COLUMN], U16, name="idx2")
+        idx3 = lists.tile([P, M_OUT // PER_COLUMN], U16, name="idx3")
 
         def entries(idx, cols):
-            return idx[:, cols.start // 16 : cols.stop // 16]
+            return idx[:, cols.start // PER_COLUMN : cols.stop // PER_COLUMN]
 
-        def held(shape, dtype, name, tag=None):
-            return keep.tile(shape, dtype, name=name, tag=tag or name, align_bytes=64)
+        def held(shape, dtype, name, reuse=None):
+            return keep.tile(shape, dtype, name=name, tag=reuse or name, align_bytes=64)
 
-        tab_w = [held([P, T], U32, f"tab_w{a}") for a in range(2)]
-        tab_s = held([P, 2, T], U8, "tab_s")
-        w1s_raw = held([P, 2, H], U8, "w1s_raw")
+        tab_w = [held([P, T], U32, f"tab_w{a}") for a in range(PASSES)]
+        tab_s = held([P, PASSES, T], U8, "tab_s")
+        w1s_raw = held([P, PASSES, H], U8, "w1s_raw")
         w4s_raw = held([P, N], U8, "w4s_raw")
-        w1_raw = [held([P, 2, 2 * KP], U8, f"w1_raw{b}") for b in range(2)]
-        w4_raw = held([P, 2, N], U32, "w4_raw")
-        w2_raw = [[held([P, PACK, KP], F32, f"w2_raw{b}{a}") for a in range(2)] for b in range(2)]
-        w3_raw = [held([P, PACK, N], F32, f"w3_raw{b}") for b in range(2)]
+        w1_raw = [held([P, PASSES, 2 * KP], U8, f"w1_raw{b}") for b in range(PASSES)]
+        w4_raw = held([P, PASSES, N], U32, "w4_raw")
+        w2_raw = [[held([P, PACK, KP], F32, f"w2_raw{b}{a}") for a in range(PASSES)] for b in range(PASSES)]
+        w3_raw = [held([P, PACK, N], F32, f"w3_raw{b}") for b in range(PASSES)]
         h = [held([P, S], F32, f"h{i}") for i in range(TILES)]
         page = [held([P, T2], F32, f"page{i}") for i in range(TILES)]
         wgs_raw = held([P, S], F32, "wgs_raw")
         wg = [held([P, S], F32, f"wg{t}") for t in range(PACK)]
         ident = held([P, P], F32, "ident")
         make_identity(nc, ident[:])
-        gain_t = held([P, 2, PACK], F32, "gain_t")
+        gain_t = held([P, PASSES, PACK], F32, "gain_t")
 
         nc.vector.memset(tab_s[:].rearrange("p a n -> p (a n)").bitcast(I32), 0)
         nc.vector.memset(w1s_raw[:].rearrange("p a n -> p (a n)").bitcast(I32), 0)
         nc.vector.memset(w4s_raw[:].bitcast(I32), 0)
 
         def load_w2(b, a):
-            src = w2[KP * a : KP * (a + 1), KP * b : KP * (b + 1)].rearrange("(p j) c -> p j c", j=PACK)
+            src = w2[KP * a : KP * (a + 1), KP * b : KP * (b + 1)].rearrange("(p u) n -> p u n", u=PACK)
             nc.sync.dma_start(out=w2_raw[b][a][:], in_=src)
 
         def load_w3(b):
-            src = w3[KP * b : KP * (b + 1), :].rearrange("(p j) c -> p j c", j=PACK)
+            src = w3[KP * b : KP * (b + 1), :].rearrange("(p u) n -> p u n", u=PACK)
             nc.sync.dma_start(out=w3_raw[b][:], in_=src)
 
         def load_tab(a):
-            src = tab_words[a].rearrange("p n i -> p (n i)").bitcast(I32)
+            src = tab_words[a].rearrange("p n u -> p (n u)").bitcast(I32)
             nc.sync.dma_start(out=tab_w[a][:].bitcast(I32), in_=src)
 
-        def load_scale_rows(queue, dst, src):
-            for q in range(4):
-                rows = src[:, 4 * q : 4 * q + 4, :].rearrange("a r n -> r a n").bitcast(I32)
-                queue.dma_start(out=dst[32 * q : 32 * q + 4, :, :].bitcast(I32), in_=rows)
+        def load_scale_rows(dst, src):
+            for quad in range(QUADS):
+                rows = src[:, 4 * quad : 4 * quad + 4, :].rearrange("a s n -> s a n").bitcast(I32)
+                nc.sync.dma_start(out=dst[QUAD * quad : QUAD * quad + 4, :, :].bitcast(I32), in_=rows)
 
         def load_w1(b):
-            src = w1_words[:, :, 2 * KP * b : 2 * KP * (b + 1)].rearrange("a p c -> p a c").bitcast(I32)
+            src = w1_words[:, :, 2 * KP * b : 2 * KP * (b + 1)].rearrange("a p n -> p a n").bitcast(I32)
             nc.sync.dma_start(out=w1_raw[b][:].bitcast(I32), in_=src)
 
         def rows_of(mat, i):
             b, t = divmod(i, PACK)
-            return mat[KP * b : KP * (b + 1), :].rearrange("(p t) c -> p t c", t=PACK)[:, t, :]
+            return mat[KP * b : KP * (b + 1), :].rearrange("(p t) n -> p t n", t=PACK)[:, t, :]
 
         def load_rows(i):
             nc.sync.dma_start(out=page[i][:], in_=rows_of(page0, i))
@@ -102,17 +109,17 @@ def tile_list_trail_erosion_closure_kernel(
         nc.sync.dma_start(idx1[:], offs)
         nc.sync.dma_start(out=wgs_raw[:], in_=wgs)
         nc.sync.dma_start(idx2[:], offs2)
-        load_scale_rows(nc.sync, tab_s, tab_scales)
+        load_scale_rows(tab_s, tab_scales)
         load_w2(0, 0)
         load_w2(0, 1)
-        load_scale_rows(nc.sync, w1s_raw, w1_scales)
+        load_scale_rows(w1s_raw, w1_scales)
         load_w1(0)
         load_tab(0)
         load_tab(1)
         nc.sync.dma_start(out=h[0][:], in_=rows_of(slope, 0))
         load_rows(0)
         nc.sync.dma_start(idx3[:], offs3)
-        nc.sync.dma_start(out=gain_t[:], in_=gain.rearrange("(b p t) -> p b t", b=2, t=PACK))
+        nc.sync.dma_start(out=gain_t[:], in_=gain.rearrange("(b p t) -> p b t", b=PASSES, t=PACK))
         load_rows(1)
         load_w2(1, 0)
         load_rows(2)
@@ -124,82 +131,82 @@ def tile_list_trail_erosion_closure_kernel(
         load_w3(1)
         nc.sync.dma_start(
             out=w4_raw[:].bitcast(I32),
-            in_=w4_words.rearrange("a p c i -> p a (c i)").bitcast(I32),
+            in_=w4_words.rearrange("a p n u -> p a (n u)").bitcast(I32),
         )
-        for q in range(4):
+        for quad in range(QUADS):
             nc.sync.dma_start(
-                out=w4s_raw[32 * q : 32 * q + 8, :].bitcast(I32),
-                in_=w4_scales[:, 4 * q : 4 * q + 4, :].bitcast(I32),
+                out=w4s_raw[QUAD * quad : QUAD * quad + 4 * PASSES, :].bitcast(I32),
+                in_=w4_scales[:, 4 * quad : 4 * quad + 4, :].bitcast(I32),
             )
         for i in range(5, TILES):
             load_rows(i)
 
-        wgs_turned = psum.tile([P, S // P, P], F32, name="wgs_turned", tag="bank2")
+        wgs_turned = psum.tile([P, S // P, P], F32, name="wgs_turned", tag=f"bank{TURNED_BANK}")
         for c in range(S // P):
             nc.tensor.transpose(wgs_turned[:, c, :], wgs_raw[:, P * c : P * (c + 1)], ident[:])
 
-        def spread_wg(t, tag):
-            rows = wgs_turned[:].rearrange("p c (q t) -> p c t q", t=PACK)[:, :, t : t + 1, :]
-            repeated = held([P, S // P, 4, 32], F32, f"wg_rep{t}", tag=tag)
-            nc.scalar.copy(out=repeated[:], in_=rows.to_broadcast([P, S // P, 4, 32]))
-            back = psum.tile([P, S // P, P], F32, name=f"wg_back{t}", tag=f"bank{3 + t % 2}")
+        def spread_wg(t, reuse):
+            picked = wgs_turned[:].rearrange("p c (q t) -> p c t q", t=PACK)[:, :, t : t + 1, :]
+            repeated = held([P, S // P, QUADS, QUAD], F32, f"wg_rep{t}", reuse)
+            nc.scalar.copy(out=repeated[:], in_=picked.to_broadcast([P, S // P, QUADS, QUAD]))
+            back = psum.tile([P, S // P, P], F32, name=f"wg_back{t}", tag=f"bank{BACK_BANKS[t % 2]}")
             for c in range(S // P):
-                nc.tensor.transpose(back[:, c, :], repeated[:, c, :, :].rearrange("p r q -> p (r q)"), ident[:])
-            nc.scalar.copy(out=wg[t][:], in_=back[:].rearrange("p c j -> p (c j)"))
+                nc.tensor.transpose(back[:, c, :], repeated[:, c, :, :].rearrange("p d q -> p (d q)"), ident[:])
+            nc.scalar.copy(out=wg[t][:], in_=back[:].rearrange("p c n -> p (c n)"))
 
         spread_wg(0, None)
 
         def round_weight(raw, sign, name):
             rounded = ring.tile([P, PACK * KP], BF16, name=f"{name}_bf", tag="w_bf", align_bytes=64)
             nc.scalar.activation(
-                out=rounded[:].rearrange("p (t q j) -> p q j t", t=PACK, j=PACK),
-                in_=raw[:].rearrange("p j (q t) -> p q j t", t=PACK),
+                out=rounded[:].rearrange("p (t q u) -> p q u t", t=PACK, u=PACK),
+                in_=raw[:].rearrange("p u (q t) -> p q u t", t=PACK),
                 func=ACT.Copy,
                 scale=sign,
             )
             return rounded
 
-        def quantise(rounded, name, tag=None):
-            width = rounded.shape[1] // PACK
-            codes = held([P, width], U32, f"{name}_codes", tag=tag)
+        def quantise(woven, name, reuse=None):
+            width = woven.shape[1] // PACK
+            codes = held([P, width], U32, f"{name}_codes", reuse)
             scales = held([P, width], U8, f"{name}_scales")
-            nc.vector.quantize_mx(out=codes[:].bitcast(E4M3), scales=scales[:], in_=rounded[:])
+            nc.vector.quantize_mx(out=codes[:].bitcast(E4M3), scales=scales[:], in_=woven[:])
             return codes, scales
 
-        def deal(copy, dst, src):
-            copy(out=dst.rearrange("p a (t q) -> p a q t", t=PACK), in_=src.rearrange("p a (q t) -> p a q t", t=PACK))
+        def deal_words(dst, src):
+            nc.scalar.copy(
+                out=dst.rearrange("p a (t q) -> p a q t", t=PACK), in_=src.rearrange("p a (q t) -> p a q t", t=PACK)
+            )
 
         def deal_w1_words(b):
-            dealt = held([P, 2, 2 * KP], U8, f"w1_dealt{b}")
-            deal(nc.scalar.copy, dealt[:].bitcast(U16), w1_raw[b][:].bitcast(U16))
+            dealt = held([P, PASSES, 2 * KP], U8, f"w1_dealt{b}")
+            deal_words(dealt[:].bitcast(U16), w1_raw[b][:].bitcast(U16))
             return dealt
 
-        w2q = [[None, None], [None, None]]
-        w1d = [None, None]
-        v_w = [held([P, S], U32, f"v_w{a}") for a in range(2)]
-        v_s = [held([P, S], U8, f"v_s{a}") for a in range(2)]
-
-        for a in range(2):
+        v_w = [held([P, S], U32, f"v_w{a}") for a in range(PASSES)]
+        v_s = [held([P, S], U8, f"v_s{a}") for a in range(PASSES)]
+        for a in range(PASSES):
             nc.vector.tensor_copy(v_s[a][:], tab_s[:, a, :].indirect(idx1[:]))
-        w1s = held([P, 2, H], U8, "w1s")
+        w1s = held([P, PASSES, H], U8, "w1s")
         nc.vector.tensor_copy(
-            out=w1s[:].rearrange("p a (b t q) -> p (a b) t q", b=2, t=PACK),
-            in_=w1s_raw[:].rearrange("p a (b q t) -> p (a b) t q", b=2, t=PACK),
+            out=w1s[:].rearrange("p a (b t q) -> p (a b) t q", b=PASSES, t=PACK),
+            in_=w1s_raw[:].rearrange("p a (b q t) -> p (a b) t q", b=PASSES, t=PACK),
         )
-        for a in range(2):
-            w2q[0][a] = quantise(round_weight(w2_raw[0][a], -1.0, f"w2_0{a}"), f"w2_0{a}")
-        w1d[0] = deal_w1_words(0)
+        neg_w2 = {}
+        for a in range(PASSES):
+            neg_w2[0, a] = quantise(round_weight(w2_raw[0][a], -1.0, f"w2_0{a}"), f"w2_0{a}")
+        w1d = [deal_w1_words(0)]
         nc.vector.tensor_copy(v_w[0][:], tab_w[0][:].indirect(idx1[:]))
         for cols in HALVES:
             nc.vector.tensor_copy(v_w[1][:, cols], tab_w[1][:].indirect(entries(idx1, cols)))
 
         neg_top = held([P, TILES], F32, "neg_top")
-        x_rows = [held([P, PACK - b, M_OUT], BF16, f"x_rows{b}") for b in range(2)]
+        x_rows = [held([P, PACK, M_OUT], BF16, "x_rows0"), held([P, PACK - 1, M_OUT], BF16, "x_rows1")]
 
         def make_h(i, cols, bank):
             b, t = divmod(i, PACK)
             acc = psum.tile([P, cols.stop - cols.start], F32, name=f"acc{i}_{cols.start}", tag=f"bank{bank}")
-            for a in range(2):
+            for a in range(PASSES):
                 nc.tensor.matmul_mx(
                     out=acc[:],
                     lhsT=w1d[b][:, a, 2 * P * t : 2 * P * (t + 1)].bitcast(E2M1),
@@ -209,7 +216,7 @@ def tile_list_trail_erosion_closure_kernel(
                     start=(a == 0),
                     stop=False,
                 )
-                codes, scales = w2q[b][a]
+                codes, scales = neg_w2[b, a]
                 nc.tensor.matmul_mx(
                     out=acc[:],
                     lhsT=codes[:, P * t : P * (t + 1)].bitcast(E4M3),
@@ -217,7 +224,7 @@ def tile_list_trail_erosion_closure_kernel(
                     rhs=v_w[a][:, cols].bitcast(E4M3),
                     rhs_scale=v_s[a][:, cols],
                     start=False,
-                    stop=(a == 1),
+                    stop=(a == PASSES - 1),
                 )
             nc.vector.tensor_tensor(h[i][:, cols], acc[:], h[i][:, cols], ALU.mult)
 
@@ -228,54 +235,53 @@ def tile_list_trail_erosion_closure_kernel(
         def row_max(i):
             nc.vector.tensor_reduce(neg_top[:, i : i + 1], page[i][:], AX.X, ALU.max, negate=True)
 
-        def look(i, cols, tag):
-            looked = held([P, cols.stop - cols.start], F32, f"look{i}_{cols.start}", tag=tag)
+        def look(i, cols, looked):
             nc.scalar.activation(
-                out=looked[:],
+                out=looked[:, cols],
                 in_=page[i][:].indirect(entries(idx3, cols)),
                 func=ACT.Exp,
                 bias=neg_top[:, i : i + 1],
             )
-            return looked
 
-        def look_row(i, tag):
+        def look_row(i, reuse):
             b, t = divmod(i, PACK)
-            looked = look(i, WHOLE, tag)
+            looked = held([P, M_OUT], F32, f"look{i}", reuse)
+            look(i, WHOLE, looked)
             nc.scalar.activation(out=x_rows[b][:, t, :], in_=looked[:], func=ACT.Copy, scale=gain_t[:, b, t : t + 1])
 
         def weave(copy, dst, src):
-            slots = src.shape[1]
             copy(
-                out=dst[:].rearrange("p (c i t) -> p c t i", t=PACK, i=4)[:, :, 0:slots, :],
-                in_=src.rearrange("p t (c i) -> p c t i", i=4),
+                out=dst[:].rearrange("p (g e t) -> p g t e", t=PACK, e=RUN)[:, :, 0 : src.shape[1], :],
+                in_=src.rearrange("p t (g e) -> p g t e", e=RUN),
             )
 
-        def step(i, tag):
+        def step(i, look_reuses):
             scatter(i, WHOLE)
-            make_h(i + 1, WHOLE, 6 + i % 2)
+            make_h(i + 1, WHOLE, FIRST_STAGE_BANKS[i % 2])
             row_max(i)
-            look_row(i, tag)
+            look_row(i, look_reuses)
 
         for half, cols in enumerate(HALVES):
-            make_h(0, cols, 6 + half)
+            make_h(0, cols, FIRST_STAGE_BANKS[half])
             scatter(0, cols)
-        make_h(1, WHOLE, 6)
+        make_h(1, WHOLE, FIRST_STAGE_BANKS[0])
         for t in range(1, PACK):
             spread_wg(t, "tab_w1")
         row_max(0)
-        look_row(0, None)
+
         w2_10 = round_weight(w2_raw[1][0], -1.0, "w2_10")
-        step(1, "w2_raw10")
+        look_row(0, "w2_raw10")
         w2_11 = round_weight(w2_raw[1][1], -1.0, "w2_11")
-        w1d[1] = deal_w1_words(1)
-        step(2, "w2_raw11")
-        w2q[1][0] = quantise(w2_10, "w2_10", tag="h1")
-        w2q[1][1] = quantise(w2_11, "w2_11", tag="h2")
+        w1d.append(deal_w1_words(1))
+        step(1, "w1_raw1")
+        neg_w2[1, 0] = quantise(w2_10, "w2_10", "h1")
         w3_0 = round_weight(w3_raw[0], 1.0, "w3_0")
-        step(3, "w3_raw0")
+        step(2, "w3_raw0")
+        neg_w2[1, 1] = quantise(w2_11, "w2_11", "h2")
         w3_1 = round_weight(w3_raw[1], 1.0, "w3_1")
-        w4d = held([P, 2, N], U32, "w4d")
-        deal(nc.scalar.copy, w4d[:], w4_raw[:])
+        step(3, "w3_raw1")
+        w4d = held([P, PASSES, N], U32, "w4d")
+        deal_words(w4d[:], w4_raw[:])
         w4s = held([P, N], U8, "w4s")
         nc.vector.tensor_copy(
             out=w4s[:].rearrange("p (t q) -> p t q", t=PACK),
@@ -283,16 +289,17 @@ def tile_list_trail_erosion_closure_kernel(
         )
         x0_bf = held([P, PACK * M_OUT], BF16, "x0_bf")
         weave(nc.scalar.copy, x0_bf, x_rows[0][:])
-        step(4, "w3_raw1")
-        w3q = [quantise(w3_0, "w3_0", tag="h4")]
+        step(4, "w3_raw0")
+        w3q = [quantise(w3_0, "w3_0", "h4")]
         step(5, "w2_raw10")
-        w3q.append(quantise(w3_1, "w3_1", tag="h5"))
+        w3q.append(quantise(w3_1, "w3_1", "h5"))
         step(6, "w2_raw11")
         x1_bf = [held([P, PACK * HALF], BF16, f"x1_bf{half}") for half in range(2)]
         for half, cols in enumerate(HALVES):
             weave(nc.scalar.copy, x1_bf[half], x_rows[1][:, :, cols])
         scatter(LAST, WHOLE)
-        x0_codes = held([P, M_OUT], U32, "x0_codes", tag=f"h{LAST}")
+
+        x0_codes = held([P, M_OUT], U32, "x0_codes", f"h{LAST}")
         x0_scales = held([P, M_OUT], U8, "x0_scales")
 
         def quantise_x0(cols):
@@ -306,40 +313,45 @@ def tile_list_trail_erosion_closure_kernel(
         row_max(LAST)
         quantise_x0(HALVES[1])
 
-        banks = {}
+        sums = {}
 
         def second_stage(b, half, x_codes, x_scales):
-            for u in range(2):
-                for w in range(2):
+            for pair in range(2):
+                for weight in range(2):
                     if b == 0:
-                        banks[half, u, w] = psum.tile(
-                            [P, 2, HALF], F32, name=f"y{half}{u}{w}", tag=f"bank{4 * half + 2 * u + w}"
+                        sums[half, pair, weight] = psum.tile(
+                            [P, 2, HALF],
+                            F32,
+                            name=f"sums{half}{pair}{weight}",
+                            tag=f"bank{4 * half + 2 * pair + weight}",
                         )
-                    for e in range(2):
-                        cols = slice(P * (2 * u + e), P * (2 * u + e + 1))
-                        if w == 0:
-                            codes, scales = w3q[b][0][:, cols], w3q[b][1][:, cols]
+                    for side in range(2):
+                        t = 2 * pair + side
+                        places = slice(P * t, P * (t + 1))
+                        if weight == 0:
+                            codes, scales = w3q[b][0][:, places], w3q[b][1][:, places]
                         else:
-                            codes, scales = w4d[:, b, cols], w4s[4 * b : P, cols]
+                            codes, scales = w4d[:, b, places], w4s[4 * b : P, places]
                         nc.tensor.matmul_mx(
-                            out=banks[half, u, w][:, e, :],
+                            out=sums[half, pair, weight][:, side, :],
                             lhsT=codes.bitcast(E4M3),
                             lhsT_scale=scales,
                             rhs=x_codes.bitcast(E4M3),
                             rhs_scale=x_scales,
-                            start=(b == 0 and e == 0),
-                            stop=(b == 1 and e == 1),
+                            start=(b == 0 and side == 0),
+                            stop=(b == PASSES - 1 and side == 1),
                         )
 
         for half, cols in enumerate(HALVES):
             second_stage(0, half, x0_codes[:, cols], x0_scales[:, cols])
 
+        looked_last = held([P, M_OUT], F32, "look_last", "x_rows1")
         for half, cols in enumerate(HALVES):
-            looked = look(LAST, cols, None)
+            look(LAST, cols, looked_last)
             nc.vector.tensor_scalar(
-                x1_bf[half][:].rearrange("p (m t) -> p m t", t=PACK)[:, :, PACK - 1],
-                looked[:],
-                gain_t[:, 1, PACK - 1 : PACK],
+                x1_bf[half][:].rearrange("p (n t) -> p n t", t=PACK)[:, :, PACK - 1],
+                looked_last[:, cols],
+                gain_t[:, PASSES - 1, PACK - 1 : PACK],
                 None,
                 ALU.mult,
             )
@@ -348,11 +360,12 @@ def tile_list_trail_erosion_closure_kernel(
 
         y = [held([P, PACK, HALF], F32, f"y{half}") for half in range(2)]
         for half, cols in enumerate(HALVES):
-            for u in range(2):
-                y3 = ring.tile([P, 2, HALF], F32, name=f"y3_{half}{u}", tag="y3")
-                nc.scalar.copy(out=y3[:], in_=banks[half, u, 0][:])
-                nc.vector.tensor_tensor(y[half][:, 2 * u : 2 * u + 2, :], banks[half, u, 1][:], y3[:], ALU.mult)
-            nc.sync.dma_start(out=out_0.rearrange("(p t) m -> p t m", t=PACK)[:, :, cols], in_=y[half][:])
+            for pair in range(2):
+                y3 = ring.tile([P, 2, HALF], F32, name=f"y3_{half}{pair}", tag="y3")
+                nc.scalar.copy(out=y3[:], in_=sums[half, pair, 0][:])
+                nc.vector.tensor_tensor(y[half][:, 2 * pair : 2 * pair + 2, :], sums[half, pair, 1][:], y3[:], ALU.mult)
+            nc.sync.dma_start(out=out_0.rearrange("(p t) n -> p t n", t=PACK)[:, :, cols], in_=y[half][:])
+
         y_bf = [held([P, PACK * HALF], BF16, f"y_bf{half}") for half in range(2)]
         weave(nc.scalar.copy, y_bf[0], y[0][:])
         weave(nc.vector.tensor_copy, y_bf[1], y[1][:])
@@ -361,10 +374,11 @@ def tile_list_trail_erosion_closure_kernel(
             y_codes = held([P, HALF], U32, f"y_codes{half}")
             nc.vector.quantize_mx(out=y_codes[:].bitcast(E4M3), scales=y_scales[:, cols], in_=y_bf[half][:])
             nc.sync.dma_start(
-                out=out_1[0].rearrange("p m i -> p (m i)").bitcast(I32)[:, cols], in_=y_codes[:].bitcast(I32)
+                out=out_1[0].rearrange("p n u -> p (n u)").bitcast(I32)[:, cols], in_=y_codes[:].bitcast(I32)
             )
-        for q in range(4):
-            queue = nc.scalar if q % 2 else nc.sync
+        for quad in range(QUADS):
+            queue = nc.scalar if quad % 2 else nc.sync
             queue.dma_start(
-                out=out_2[0, 4 * q : 4 * q + 4, :].bitcast(I32), in_=y_scales[32 * q : 32 * q + 4, :].bitcast(I32)
+                out=out_2[0, 4 * quad : 4 * quad + 4, :].bitcast(I32),
+                in_=y_scales[QUAD * quad : QUAD * quad + 4, :].bitcast(I32),
             )

from contextlib import ExitStack

import concourse.mybir as mybir
from concourse.masks import make_identity

K, T, S, T2, M_OUT, H, N = 1024, 2048, 512, 1024, 512, 1024, 512
FLOPS = 2 * (2 * K * H * S + 2 * H * N * M_OUT)

F32 = mybir.dt.float32
BF16 = mybir.dt.bfloat16
I32 = mybir.dt.int32
U32 = mybir.dt.uint32
U16 = mybir.dt.uint16
U8 = mybir.dt.uint8
E4M3 = mybir.dt.float8_e4m3fn_x4
E2M1 = mybir.dt.float4_e2m1fn_x4
ACT = mybir.ActivationFunctionType
ALU = mybir.AluOpType
AX = mybir.AxisListType

P = 128
PACK = 4
KP = P * PACK
PASSES = 2
QUADS, QUAD = 4, 32
PER_COLUMN = 16
RUN = 4
TILES = H // P
LAST = TILES - 1
HALF = 256
WHOLE = slice(0, 2 * HALF)
HALVES = (slice(0, HALF), slice(HALF, 2 * HALF))
FIRST_STAGE_BANKS = (6, 7)
TURNED_BANK = 2
BACK_BANKS = (3, 4)


def tile_list_trail_erosion_closure_kernel(
    tc, tab_words, tab_scales, offs, offs2, offs3, w1_words, w1_scales, w2,
    slope, page0, wgs, gain, w3, w4_words, w4_scales, out_0, out_1, out_2,
):
    nc = tc.nc
    with ExitStack() as ctx:
        lists = ctx.enter_context(tc.tile_pool(name="lists", bufs=1))
        keep = ctx.enter_context(tc.tile_pool(name="keep", bufs=1))
        ring = ctx.enter_context(tc.tile_pool(name="ring", bufs=2))
        psum = ctx.enter_context(tc.psum_pool(name="psum", bufs=1))

        idx1 = lists.tile([P, S // PER_COLUMN], U16, name="idx1")
        idx2 = lists.tile([P, S // PER_COLUMN], U16, name="idx2")
        idx3 = lists.tile([P, M_OUT // PER_COLUMN], U16, name="idx3")

        def entries(idx, cols):
            return idx[:, cols.start // PER_COLUMN : cols.stop // PER_COLUMN]

        def held(shape, dtype, name, reuse=None):
            return keep.tile(shape, dtype, name=name, tag=reuse or name, align_bytes=64)

        tab_w = [held([P, T], U32, f"tab_w{a}") for a in range(PASSES)]
        tab_s = held([P, PASSES, T], U8, "tab_s")
        w1s_raw = held([P, PASSES, H], U8, "w1s_raw")
        w4s_raw = held([P, N], U8, "w4s_raw")
        w1_raw = [held([P, PASSES, 2 * KP], U8, f"w1_raw{b}") for b in range(PASSES)]
        w4_raw = held([P, PASSES, N], U32, "w4_raw")
        w2_raw = [[held([P, PACK, KP], F32, f"w2_raw{b}{a}") for a in range(PASSES)] for b in range(PASSES)]
        w3_raw = [held([P, PACK, N], F32, f"w3_raw{b}") for b in range(PASSES)]
        h = [held([P, S], F32, f"h{i}") for i in range(TILES)]
        page = [held([P, T2], F32, f"page{i}") for i in range(TILES)]
        wgs_raw = held([P, S], F32, "wgs_raw")
        wg = [held([P, S], F32, f"wg{t}") for t in range(PACK)]
        ident = held([P, P], F32, "ident")
        make_identity(nc, ident[:])
        gain_t = held([P, PASSES, PACK], F32, "gain_t")

        nc.vector.memset(tab_s[:].rearrange("p a n -> p (a n)").bitcast(I32), 0)
        nc.vector.memset(w1s_raw[:].rearrange("p a n -> p (a n)").bitcast(I32), 0)
        nc.vector.memset(w4s_raw[:].bitcast(I32), 0)

        def load_w2(b, a):
            src = w2[KP * a : KP * (a + 1), KP * b : KP * (b + 1)].rearrange("(p u) n -> p u n", u=PACK)
            nc.sync.dma_start(out=w2_raw[b][a][:], in_=src)

        def load_w3(b):
            src = w3[KP * b : KP * (b + 1), :].rearrange("(p u) n -> p u n", u=PACK)
            nc.sync.dma_start(out=w3_raw[b][:], in_=src)

        def load_tab(a):
            src = tab_words[a].rearrange("p n u -> p (n u)").bitcast(I32)
            nc.sync.dma_start(out=tab_w[a][:].bitcast(I32), in_=src)

        def load_scale_rows(dst, src):
            for quad in range(QUADS):
                rows = src[:, 4 * quad : 4 * quad + 4, :].rearrange("a s n -> s a n").bitcast(I32)
                nc.sync.dma_start(out=dst[QUAD * quad : QUAD * quad + 4, :, :].bitcast(I32), in_=rows)

        def load_w1(b):
            src = w1_words[:, :, 2 * KP * b : 2 * KP * (b + 1)].rearrange("a p n -> p a n").bitcast(I32)
            nc.sync.dma_start(out=w1_raw[b][:].bitcast(I32), in_=src)

        def rows_of(mat, i):
            b, t = divmod(i, PACK)
            return mat[KP * b : KP * (b + 1), :].rearrange("(p t) n -> p t n", t=PACK)[:, t, :]

        def load_rows(i):
            nc.sync.dma_start(out=page[i][:], in_=rows_of(page0, i))
            if i < LAST:
                nc.sync.dma_start(out=h[i + 1][:], in_=rows_of(slope, i + 1))

        nc.sync.dma_start(idx1[:], offs)
        nc.sync.dma_start(out=wgs_raw[:], in_=wgs)
        nc.sync.dma_start(idx2[:], offs2)
        load_scale_rows(tab_s, tab_scales)
        load_w2(0, 0)
        load_w2(0, 1)
        load_scale_rows(w1s_raw, w1_scales)
        load_w1(0)
        load_tab(0)
        load_tab(1)
        nc.sync.dma_start(out=h[0][:], in_=rows_of(slope, 0))
        load_rows(0)
        nc.sync.dma_start(idx3[:], offs3)
        nc.sync.dma_start(out=gain_t[:], in_=gain.rearrange("(b p t) -> p b t", b=PASSES, t=PACK))
        load_rows(1)
        load_w2(1, 0)
        load_rows(2)
        load_w2(1, 1)
        load_w1(1)
        load_w3(0)
        load_rows(3)
        load_rows(4)
        load_w3(1)
        nc.sync.dma_start(
            out=w4_raw[:].bitcast(I32),
            in_=w4_words.rearrange("a p n u -> p a (n u)").bitcast(I32),
        )
        for quad in range(QUADS):
            nc.sync.dma_start(
                out=w4s_raw[QUAD * quad : QUAD * quad + 4 * PASSES, :].bitcast(I32),
                in_=w4_scales[:, 4 * quad : 4 * quad + 4, :].bitcast(I32),
            )
        for i in range(5, TILES):
            load_rows(i)

        wgs_turned = psum.tile([P, S // P, P], F32, name="wgs_turned", tag=f"bank{TURNED_BANK}")
        for c in range(S // P):
            nc.tensor.transpose(wgs_turned[:, c, :], wgs_raw[:, P * c : P * (c + 1)], ident[:])

        def spread_wg(t, reuse):
            picked = wgs_turned[:].rearrange("p c (q t) -> p c t q", t=PACK)[:, :, t : t + 1, :]
            repeated = held([P, S // P, QUADS, QUAD], F32, f"wg_rep{t}", reuse)
            nc.scalar.copy(out=repeated[:], in_=picked.to_broadcast([P, S // P, QUADS, QUAD]))
            back = psum.tile([P, S // P, P], F32, name=f"wg_back{t}", tag=f"bank{BACK_BANKS[t % 2]}")
            for c in range(S // P):
                nc.tensor.transpose(back[:, c, :], repeated[:, c, :, :].rearrange("p d q -> p (d q)"), ident[:])
            nc.scalar.copy(out=wg[t][:], in_=back[:].rearrange("p c n -> p (c n)"))

        spread_wg(0, None)

        def round_weight(raw, sign, name):
            rounded = ring.tile([P, PACK * KP], BF16, name=f"{name}_bf", tag="w_bf", align_bytes=64)
            nc.scalar.activation(
                out=rounded[:].rearrange("p (t q u) -> p q u t", t=PACK, u=PACK),
                in_=raw[:].rearrange("p u (q t) -> p q u t", t=PACK),
                func=ACT.Copy,
                scale=sign,
            )
            return rounded

        def quantise(woven, name, reuse=None):
            width = woven.shape[1] // PACK
            codes = held([P, width], U32, f"{name}_codes", reuse)
            scales = held([P, width], U8, f"{name}_scales")
            nc.vector.quantize_mx(out=codes[:].bitcast(E4M3), scales=scales[:], in_=woven[:])
            return codes, scales

        def deal_words(dst, src):
            nc.scalar.copy(
                out=dst.rearrange("p a (t q) -> p a q t", t=PACK), in_=src.rearrange("p a (q t) -> p a q t", t=PACK)
            )

        def deal_w1_words(b):
            dealt = held([P, PASSES, 2 * KP], U8, f"w1_dealt{b}")
            deal_words(dealt[:].bitcast(U16), w1_raw[b][:].bitcast(U16))
            return dealt

        v_w = [held([P, S], U32, f"v_w{a}") for a in range(PASSES)]
        v_s = [held([P, S], U8, f"v_s{a}") for a in range(PASSES)]
        for a in range(PASSES):
            nc.vector.tensor_copy(v_s[a][:], tab_s[:, a, :].indirect(idx1[:]))
        w1s = held([P, PASSES, H], U8, "w1s")
        nc.vector.tensor_copy(
            out=w1s[:].rearrange("p a (b t q) -> p (a b) t q", b=PASSES, t=PACK),
            in_=w1s_raw[:].rearrange("p a (b q t) -> p (a b) t q", b=PASSES, t=PACK),
        )
        neg_w2 = {}
        for a in range(PASSES):
            neg_w2[0, a] = quantise(round_weight(w2_raw[0][a], -1.0, f"w2_0{a}"), f"w2_0{a}")
        w1d = [deal_w1_words(0)]
        nc.vector.tensor_copy(v_w[0][:], tab_w[0][:].indirect(idx1[:]))
        for cols in HALVES:
            nc.vector.tensor_copy(v_w[1][:, cols], tab_w[1][:].indirect(entries(idx1, cols)))

        neg_top = held([P, TILES], F32, "neg_top")
        x_rows = [held([P, PACK, M_OUT], BF16, "x_rows0"), held([P, PACK - 1, M_OUT], BF16, "x_rows1")]

        def make_h(i, cols, bank):
            b, t = divmod(i, PACK)
            acc = psum.tile([P, cols.stop - cols.start], F32, name=f"acc{i}_{cols.start}", tag=f"bank{bank}")
            for a in range(PASSES):
                nc.tensor.matmul_mx(
                    out=acc[:],
                    lhsT=w1d[b][:, a, 2 * P * t : 2 * P * (t + 1)].bitcast(E2M1),
                    lhsT_scale=w1s[:, a, KP * b + P * t : KP * b + P * (t + 1)],
                    rhs=v_w[a][:, cols].bitcast(E4M3),
                    rhs_scale=v_s[a][:, cols],
                    start=(a == 0),
                    stop=False,
                )
                codes, scales = neg_w2[b, a]
                nc.tensor.matmul_mx(
                    out=acc[:],
                    lhsT=codes[:, P * t : P * (t + 1)].bitcast(E4M3),
                    lhsT_scale=scales[:, P * t : P * (t + 1)],
                    rhs=v_w[a][:, cols].bitcast(E4M3),
                    rhs_scale=v_s[a][:, cols],
                    start=False,
                    stop=(a == PASSES - 1),
                )
            nc.vector.tensor_tensor(h[i][:, cols], acc[:], h[i][:, cols], ALU.mult)

        def scatter(i, cols):
            window = page[i][:].indirect(entries(idx2, cols))
            nc.vector.tensor_tensor(window, h[i][:, cols], wg[i % PACK][:, cols], ALU.mult)

        def row_max(i):
            nc.vector.tensor_reduce(neg_top[:, i : i + 1], page[i][:], AX.X, ALU.max, negate=True)

        def look(i, cols, looked):
            nc.scalar.activation(
                out=looked[:, cols],
                in_=page[i][:].indirect(entries(idx3, cols)),
                func=ACT.Exp,
                bias=neg_top[:, i : i + 1],
            )

        def look_row(i, reuse):
            b, t = divmod(i, PACK)
            looked = held([P, M_OUT], F32, f"look{i}", reuse)
            look(i, WHOLE, looked)
            nc.scalar.activation(out=x_rows[b][:, t, :], in_=looked[:], func=ACT.Copy, scale=gain_t[:, b, t : t + 1])

        def weave(copy, dst, src):
            copy(
                out=dst[:].rearrange("p (g e t) -> p g t e", t=PACK, e=RUN)[:, :, 0 : src.shape[1], :],
                in_=src.rearrange("p t (g e) -> p g t e", e=RUN),
            )

        def step(i, look_reuses):
            scatter(i, WHOLE)
            make_h(i + 1, WHOLE, FIRST_STAGE_BANKS[i % 2])
            row_max(i)
            look_row(i, look_reuses)

        for half, cols in enumerate(HALVES):
            make_h(0, cols, FIRST_STAGE_BANKS[half])
            scatter(0, cols)
        make_h(1, WHOLE, FIRST_STAGE_BANKS[0])
        for t in range(1, PACK):
            spread_wg(t, "tab_w1")
        row_max(0)

        w2_10 = round_weight(w2_raw[1][0], -1.0, "w2_10")
        look_row(0, "w2_raw10")
        w2_11 = round_weight(w2_raw[1][1], -1.0, "w2_11")
        w1d.append(deal_w1_words(1))
        step(1, "w1_raw1")
        neg_w2[1, 0] = quantise(w2_10, "w2_10", "h1")
        w3_0 = round_weight(w3_raw[0], 1.0, "w3_0")
        step(2, "w3_raw0")
        neg_w2[1, 1] = quantise(w2_11, "w2_11", "h2")
        w3_1 = round_weight(w3_raw[1], 1.0, "w3_1")
        step(3, "w3_raw1")
        w4d = held([P, PASSES, N], U32, "w4d")
        deal_words(w4d[:], w4_raw[:])
        w4s = held([P, N], U8, "w4s")
        nc.vector.tensor_copy(
            out=w4s[:].rearrange("p (t q) -> p t q", t=PACK),
            in_=w4s_raw[:].rearrange("p (q t) -> p t q", t=PACK),
        )
        x0_bf = held([P, PACK * M_OUT], BF16, "x0_bf")
        weave(nc.scalar.copy, x0_bf, x_rows[0][:])
        step(4, "w3_raw0")
        w3q = [quantise(w3_0, "w3_0", "h4")]
        step(5, "w2_raw10")
        w3q.append(quantise(w3_1, "w3_1", "h5"))
        step(6, "w2_raw11")
        x1_bf = [held([P, PACK * HALF], BF16, f"x1_bf{half}") for half in range(2)]
        for half, cols in enumerate(HALVES):
            weave(nc.scalar.copy, x1_bf[half], x_rows[1][:, :, cols])
        scatter(LAST, WHOLE)

        x0_codes = held([P, M_OUT], U32, "x0_codes", f"h{LAST}")
        x0_scales = held([P, M_OUT], U8, "x0_scales")

        def quantise_x0(cols):
            nc.vector.quantize_mx(
                out=x0_codes[:, cols].bitcast(E4M3),
                scales=x0_scales[:, cols],
                in_=x0_bf[:, PACK * cols.start : PACK * cols.stop],
            )

        quantise_x0(HALVES[0])
        row_max(LAST)
        quantise_x0(HALVES[1])

        sums = {}

        def second_stage(b, half, x_codes, x_scales):
            for pair in range(2):
                for weight in range(2):
                    if b == 0:
                        sums[half, pair, weight] = psum.tile(
                            [P, 2, HALF],
                            F32,
                            name=f"sums{half}{pair}{weight}",
                            tag=f"bank{4 * half + 2 * pair + weight}",
                        )
                    for side in range(2):
                        t = 2 * pair + side
                        places = slice(P * t, P * (t + 1))
                        if weight == 0:
                            codes, scales = w3q[b][0][:, places], w3q[b][1][:, places]
                        else:
                            codes, scales = w4d[:, b, places], w4s[4 * b : P, places]
                        nc.tensor.matmul_mx(
                            out=sums[half, pair, weight][:, side, :],
                            lhsT=codes.bitcast(E4M3),
                            lhsT_scale=scales,
                            rhs=x_codes.bitcast(E4M3),
                            rhs_scale=x_scales,
                            start=(b == 0 and side == 0),
                            stop=(b == PASSES - 1 and side == 1),
                        )

        for half, cols in enumerate(HALVES):
            second_stage(0, half, x0_codes[:, cols], x0_scales[:, cols])

        looked_last = held([P, M_OUT], F32, "look_last", "x_rows1")
        for half, cols in enumerate(HALVES):
            look(LAST, cols, looked_last)
            nc.vector.tensor_scalar(
                x1_bf[half][:].rearrange("p (n t) -> p n t", t=PACK)[:, :, PACK - 1],
                looked_last[:, cols],
                gain_t[:, PASSES - 1, PACK - 1 : PACK],
                None,
                ALU.mult,
            )
            x1_codes, x1_scales = quantise(x1_bf[half], f"x1_{half}")
            second_stage(1, half, x1_codes[:], x1_scales[:])

        y = [held([P, PACK, HALF], F32, f"y{half}") for half in range(2)]
        for half, cols in enumerate(HALVES):
            for pair in range(2):
                y3 = ring.tile([P, 2, HALF], F32, name=f"y3_{half}{pair}", tag="y3")
                nc.scalar.copy(out=y3[:], in_=sums[half, pair, 0][:])
                nc.vector.tensor_tensor(y[half][:, 2 * pair : 2 * pair + 2, :], sums[half, pair, 1][:], y3[:], ALU.mult)
            nc.sync.dma_start(out=out_0.rearrange("(p t) n -> p t n", t=PACK)[:, :, cols], in_=y[half][:])

        y_bf = [held([P, PACK * HALF], BF16, f"y_bf{half}") for half in range(2)]
        weave(nc.scalar.copy, y_bf[0], y[0][:])
        weave(nc.vector.tensor_copy, y_bf[1], y[1][:])
        y_scales = held([P, M_OUT], U8, "y_scales")
        for half, cols in enumerate(HALVES):
            y_codes = held([P, HALF], U32, f"y_codes{half}")
            nc.vector.quantize_mx(out=y_codes[:].bitcast(E4M3), scales=y_scales[:, cols], in_=y_bf[half][:])
            nc.sync.dma_start(
                out=out_1[0].rearrange("p n u -> p (n u)").bitcast(I32)[:, cols], in_=y_codes[:].bitcast(I32)
            )
        for quad in range(QUADS):
            queue = nc.scalar if quad % 2 else nc.sync
            queue.dma_start(
                out=out_2[0, 4 * quad : 4 * quad + 4, :].bitcast(I32),
                in_=y_scales[QUAD * quad : QUAD * quad + 4, :].bitcast(I32),
            )
